import numpy as np
import ml_dtypes

BF16 = ml_dtypes.bfloat16


def bf(x):
    return np.asarray(x, np.float32).astype(BF16)


def f32(x):
    return np.asarray(x, np.float32)


def f64(x):
    return np.asarray(x).astype(np.float64)


def striped(idx):
    return np.concatenate([l.reshape(-1, 16).T for l in idx])


def rows(idx, k):
    return np.tile(np.repeat(idx, 16, axis=0), (k // (16 * 8), 1))


def look(tab, idx):
    return np.take_along_axis(f64(tab), rows(idx, len(tab)), axis=1)


K, S, V, N, M = 256, 2048, 2048, 2048, 256


def setup_inputs():
    return {"tab": f32(np.random.standard_normal((2, K, S))), "th": f32(0.5 * np.random.standard_normal((K, V))), "w": bf(np.random.standard_normal((K, M)) / np.sqrt(K)), "b": f32(0.5 * np.random.standard_normal((M, 1))), "offs": striped(np.stack([np.random.permutation(S)[:N] for _ in range(8)]))}


def reference(tab, th, w, b, offs):
    idx = np.stack([g.T.reshape(-1) for g in np.split(offs, 8)])
    x = (look(tab[0], idx) >= f64(th)) * look(tab[1], idx)
    return np.maximum(f64(w).T @ x + f64(b), 0.0)

@@ -1,0 +1,66 @@
+import concourse.mybir as mybir
+
+P = 128
+GROUP = 16
+PIECE = 512
+F32, BF16, U16 = mybir.dt.float32, mybir.dt.bfloat16, mybir.dt.uint16
+ALU = mybir.AluOpType
+ACT = mybir.ActivationFunctionType
+
+FLOPS = 2 * 256 * 256 * 2048
+
+
+def tile_lookup_sel_relu_kernel(tc, tab, th, w, b, offs, out):
+    nc = tc.nc
+    rows, places = tab.shape[1], tab.shape[2]
+    outs, entries = out.shape
+    row_blocks, out_blocks, pieces = rows // P, outs // P, entries // PIECE
+
+    def block(i):
+        return slice(i * P, (i + 1) * P)
+
+    def columns(j):
+        return slice(j * PIECE, (j + 1) * PIECE)
+
+    with (
+        tc.tile_pool(name="held", bufs=1) as held,
+        tc.psum_pool(name="psum", bufs=1) as psum,
+    ):
+        lists = held.tile([P, entries // GROUP], U16, name="lists")
+        keys = [held.tile([P, places], F32, name=f"keys{r}") for r in range(row_blocks)]
+        values = [held.tile([P, places], F32, name=f"values{r}") for r in range(row_blocks)]
+        limits = [[held.tile([P, PIECE], F32, name=f"limits{r}_{j}") for j in range(pieces)] for r in range(row_blocks)]
+        weights = held.tile([P, row_blocks, outs], BF16, name="weights")
+        bias = [held.tile([P, 1], F32, name=f"bias{m}") for m in range(out_blocks)]
+        sums = [[psum.tile([P, PIECE], F32, name=f"sums{m}_{j}") for j in range(pieces)] for m in range(out_blocks)]
+
+        nc.sync.dma_start(lists[:], offs)
+        for r in range(row_blocks):
+            nc.sync.dma_start(keys[r][:], tab[0, block(r), :])
+            for j in range(pieces):
+                nc.sync.dma_start(limits[r][j][:], th[block(r), columns(j)])
+            nc.sync.dma_start(values[r][:], tab[1, block(r), :])
+        nc.sync.dma_start(weights[:], w.rearrange("(r p) m -> p r m", p=P))
+        for m in range(out_blocks):
+            nc.sync.dma_start(bias[m][:], b[block(m), :])
+
+        for r in range(row_blocks):
+            passed = [held.tile([P, PIECE], F32, name=f"passed{r}_{j}") for j in range(pieces)]
+            for j in range(pieces):
+                offsets = lists[:, j * PIECE // GROUP : (j + 1) * PIECE // GROUP]
+                nc.vector.tensor_tensor(passed[j][:], keys[r][:].indirect(offsets), limits[r][j][:], ALU.is_ge)
+            for j in range(pieces):
+                offsets = lists[:, j * PIECE // GROUP : (j + 1) * PIECE // GROUP]
+                x = held.tile([P, PIECE], F32, name=f"x{r}_{j}")
+                x_bf16 = held.tile([P, PIECE], BF16, name=f"x_bf16_{r}_{j}")
+                nc.vector.tensor_tensor(x[:], values[r][:].indirect(offsets), passed[j][:], ALU.mult)
+                nc.scalar.copy(x_bf16[:], x[:])
+                for m in range(out_blocks):
+                    nc.tensor.matmul(
+                        sums[m][j][:], weights[:, r, block(m)], x_bf16[:], start=(r == 0), stop=(r == row_blocks - 1)
+                    )
+                if r == row_blocks - 1:
+                    for m in range(out_blocks):
+                        result = held.tile([P, PIECE], F32, name=f"result{m}_{j}")
+                        nc.scalar.activation(result[:], sums[m][j][:], ACT.Relu, bias=bias[m][:])
+                        nc.sync.dma_start(out[block(m), columns(j)], result[:])

@@ -3,6 +3,7 @@ import concourse.mybir as mybir
 P = 128
 GROUP = 16
 PIECE = 512
+BANKS = 8
 F32, BF16, U16 = mybir.dt.float32, mybir.dt.bfloat16, mybir.dt.uint16
 ALU = mybir.AluOpType
 ACT = mybir.ActivationFunctionType
@@ -14,53 +15,103 @@ def tile_lookup_sel_relu_kernel(tc, tab, th, w, b, offs, out):
     nc = tc.nc
     rows, places = tab.shape[1], tab.shape[2]
     outs, entries = out.shape
-    row_blocks, out_blocks, pieces = rows // P, outs // P, entries // PIECE
+    assert rows == 2 * P and outs == 2 * P
+    pieces = [slice(s, s + PIECE) for s in range(0, entries, PIECE)]
+    early, last = pieces[:-1], pieces[-1]
+    halves = [slice(s, s + PIECE // 2) for s in range(last.start, last.stop, PIECE // 2)]
 
     def block(i):
         return slice(i * P, (i + 1) * P)
 
-    def columns(j):
-        return slice(j * PIECE, (j + 1) * PIECE)
+    def width(cols):
+        return cols.stop - cols.start
 
     with (
         tc.tile_pool(name="held", bufs=1) as held,
-        tc.psum_pool(name="psum", bufs=1) as psum,
+        tc.psum_pool(name="psum", bufs=BANKS) as psum,
     ):
         lists = held.tile([P, entries // GROUP], U16, name="lists")
-        keys = [held.tile([P, places], F32, name=f"keys{r}") for r in range(row_blocks)]
-        values = [held.tile([P, places], F32, name=f"values{r}") for r in range(row_blocks)]
-        limits = [[held.tile([P, PIECE], F32, name=f"limits{r}_{j}") for j in range(pieces)] for r in range(row_blocks)]
-        weights = held.tile([P, row_blocks, outs], BF16, name="weights")
-        bias = [held.tile([P, 1], F32, name=f"bias{m}") for m in range(out_blocks)]
-        sums = [[psum.tile([P, PIECE], F32, name=f"sums{m}_{j}") for j in range(pieces)] for m in range(out_blocks)]
+        keys = [held.tile([P, places], F32, name=f"keys{r}") for r in range(2)]
+        values = [held.tile([P, places], F32, name=f"values{r}") for r in range(2)]
+        limits = [held.tile([P, entries], F32, name=f"limits{r}") for r in range(2)]
+        passed = [held.tile([P, entries], F32, name=f"passed{r}") for r in range(2)]
+        x = [held.tile([P, entries], F32, name=f"x{r}") for r in range(2)]
+        x_bf16 = [held.tile([P, entries], BF16, name=f"x_bf16_{r}") for r in range(2)]
+        result = [held.tile([P, entries], F32, name=f"result{m}") for m in range(2)]
+        weights = held.tile([P, 2, outs], BF16, name="weights")
+        bias = [held.tile([P, 1], F32, name=f"bias{m}") for m in range(2)]
+        sums = {}
 
+        def offsets(cols):
+            return lists[:, cols.start // GROUP : cols.stop // GROUP]
+
+        def load_limits(r, cols):
+            nc.sync.dma_start(limits[r][:, cols], th[block(r), cols])
+
+        def compare(r, cols):
+            nc.vector.tensor_tensor(passed[r][:, cols], keys[r][:].indirect(offsets(cols)), limits[r][:, cols], ALU.is_ge)
+
+        def product(r, cols):
+            nc.vector.tensor_tensor(x[r][:, cols], values[r][:].indirect(offsets(cols)), passed[r][:, cols], ALU.mult)
+
+        def project(r, cols):
+            for m in range(2):
+                if r == 0:
+                    sums[m, cols.start] = psum.tile([P, width(cols)], F32, name="sums")
+                nc.tensor.matmul(
+                    sums[m, cols.start][:], weights[:, r, block(m)], x_bf16[r][:, cols], start=(r == 0), stop=(r == 1)
+                )
+
+        def relu_on_scalar(m, cols):
+            nc.scalar.activation(result[m][:, cols], sums[m, cols.start][:], ACT.Relu, bias=bias[m][:])
+            nc.sync.dma_start(out[block(m), cols], result[m][:, cols])
+
+        def relu_on_vector(m, cols):
+            nc.vector.tensor_scalar(result[m][:, cols], sums[m, cols.start][:], bias[m][:], 0.0, ALU.add, ALU.max)
+            nc.sync.dma_start(out[block(m), cols], result[m][:, cols])
+
+        nc.sync.dma_start(keys[0][:], tab[0, block(0), :])
         nc.sync.dma_start(lists[:], offs)
-        for r in range(row_blocks):
-            nc.sync.dma_start(keys[r][:], tab[0, block(r), :])
-            for j in range(pieces):
-                nc.sync.dma_start(limits[r][j][:], th[block(r), columns(j)])
-            nc.sync.dma_start(values[r][:], tab[1, block(r), :])
+        for cols in early:
+            load_limits(0, cols)
+        nc.sync.dma_start(values[0][:], tab[1, block(0), :])
+        nc.sync.dma_start(keys[1][:], tab[0, block(1), :])
+        load_limits(1, early[0])
+        load_limits(1, early[1])
+        nc.sync.dma_start(values[1][:], tab[1, block(1), :])
         nc.sync.dma_start(weights[:], w.rearrange("(r p) m -> p r m", p=P))
-        for m in range(out_blocks):
+        load_limits(1, early[2])
+        for m in range(2):
             nc.sync.dma_start(bias[m][:], b[block(m), :])
+        for r in range(2):
+            load_limits(r, last)
 
-        for r in range(row_blocks):
-            passed = [held.tile([P, PIECE], F32, name=f"passed{r}_{j}") for j in range(pieces)]
-            for j in range(pieces):
-                offsets = lists[:, j * PIECE // GROUP : (j + 1) * PIECE // GROUP]
-                nc.vector.tensor_tensor(passed[j][:], keys[r][:].indirect(offsets), limits[r][j][:], ALU.is_ge)
-            for j in range(pieces):
-                offsets = lists[:, j * PIECE // GROUP : (j + 1) * PIECE // GROUP]
-                x = held.tile([P, PIECE], F32, name=f"x{r}_{j}")
-                x_bf16 = held.tile([P, PIECE], BF16, name=f"x_bf16_{r}_{j}")
-                nc.vector.tensor_tensor(x[:], values[r][:].indirect(offsets), passed[j][:], ALU.mult)
-                nc.scalar.copy(x_bf16[:], x[:])
-                for m in range(out_blocks):
-                    nc.tensor.matmul(
-                        sums[m][j][:], weights[:, r, block(m)], x_bf16[:], start=(r == 0), stop=(r == row_blocks - 1)
-                    )
-                if r == row_blocks - 1:
-                    for m in range(out_blocks):
-                        result = held.tile([P, PIECE], F32, name=f"result{m}_{j}")
-                        nc.scalar.activation(result[:], sums[m][j][:], ACT.Relu, bias=bias[m][:])
-                        nc.sync.dma_start(out[block(m), columns(j)], result[:])
+        for cols in early:
+            compare(0, cols)
+        for cols in early:
+            product(0, cols)
+            nc.scalar.copy(x_bf16[0][:, cols], x[0][:, cols])
+            project(0, cols)
+
+        compare(1, early[0])
+        for cols, ahead in zip(early, [(1, c) for c in early[1:]] + [(0, last)]):
+            compare(*ahead)
+            product(1, cols)
+            nc.scalar.copy(x_bf16[1][:, cols], x[1][:, cols])
+            project(1, cols)
+            for m in range(2):
+                relu_on_scalar(m, cols)
+
+        compare(1, last)
+        product(0, last)
+        nc.scalar.copy(x_bf16[0][:, last], x[0][:, last])
+        for cols in halves:
+            project(0, cols)
+        for cols in halves:
+            product(1, cols)
+        nc.scalar.copy(x_bf16[1][:, halves[0]], x[1][:, halves[0]])
+        nc.vector.tensor_copy(x_bf16[1][:, halves[1]], x[1][:, halves[1]])
+        for cols in halves:
+            project(1, cols)
+            relu_on_scalar(0, cols)
+            relu_on_vector(1, cols)

@@ -15,19 +15,18 @@ def tile_lookup_sel_relu_kernel(tc, tab, th, w, b, offs, out):
     nc = tc.nc
     rows, places = tab.shape[1], tab.shape[2]
     outs, entries = out.shape
-    assert rows == 2 * P and outs == 2 * P
+    assert rows == 2 * P and outs == 2 * P and entries == 4 * PIECE
     pieces = [slice(s, s + PIECE) for s in range(0, entries, PIECE)]
     early, last = pieces[:-1], pieces[-1]
-    halves = [slice(s, s + PIECE // 2) for s in range(last.start, last.stop, PIECE // 2)]
+    cuts = [last.start, last.start + PIECE // 2, last.stop - PIECE // 4, last.stop]
+    parts = [slice(lo, hi) for lo, hi in zip(cuts, cuts[1:])]
 
     def block(i):
         return slice(i * P, (i + 1) * P)
 
-    def width(cols):
-        return cols.stop - cols.start
-
     with (
         tc.tile_pool(name="held", bufs=1) as held,
+        tc.tile_pool(name="shared", bufs=1) as shared,
         tc.psum_pool(name="psum", bufs=BANKS) as psum,
     ):
         lists = held.tile([P, entries // GROUP], U16, name="lists")
@@ -36,10 +35,10 @@ def tile_lookup_sel_relu_kernel(tc, tab, th, w, b, offs, out):
         limits = [held.tile([P, entries], F32, name=f"limits{r}") for r in range(2)]
         passed = [held.tile([P, entries], F32, name=f"passed{r}") for r in range(2)]
         x = [held.tile([P, entries], F32, name=f"x{r}") for r in range(2)]
-        x_bf16 = [held.tile([P, entries], BF16, name=f"x_bf16_{r}") for r in range(2)]
         result = [held.tile([P, entries], F32, name=f"result{m}") for m in range(2)]
         weights = held.tile([P, 2, outs], BF16, name="weights")
         bias = [held.tile([P, 1], F32, name=f"bias{m}") for m in range(2)]
+        x_bf16 = {}
         sums = {}
 
         def offsets(cols):
@@ -54,12 +53,12 @@ def tile_lookup_sel_relu_kernel(tc, tab, th, w, b, offs, out):
         def product(r, cols):
             nc.vector.tensor_tensor(x[r][:, cols], values[r][:].indirect(offsets(cols)), passed[r][:, cols], ALU.mult)
 
-        def project(r, cols):
+        def project(r, cols, opens):
             for m in range(2):
-                if r == 0:
-                    sums[m, cols.start] = psum.tile([P, width(cols)], F32, name="sums")
+                if opens:
+                    sums[m, cols.start] = psum.tile([P, cols.stop - cols.start], F32, name="sums")
                 nc.tensor.matmul(
-                    sums[m, cols.start][:], weights[:, r, block(m)], x_bf16[r][:, cols], start=(r == 0), stop=(r == 1)
+                    sums[m, cols.start][:], weights[:, r, block(m)], x_bf16[r, cols.start], start=opens, stop=not opens
                 )
 
         def relu_on_scalar(m, cols):
@@ -83,35 +82,46 @@ def tile_lookup_sel_relu_kernel(tc, tab, th, w, b, offs, out):
         load_limits(1, early[2])
         for m in range(2):
             nc.sync.dma_start(bias[m][:], b[block(m), :])
-        for r in range(2):
+        for r in (1, 0):
             load_limits(r, last)
 
         for cols in early:
             compare(0, cols)
         for cols in early:
             product(0, cols)
-            nc.scalar.copy(x_bf16[0][:, cols], x[0][:, cols])
-            project(0, cols)
+            rounded = held.tile([P, PIECE], BF16, name=f"rounded0_{cols.start}")
+            x_bf16[0, cols.start] = rounded[:]
+            nc.scalar.copy(rounded[:], x[0][:, cols])
+            project(0, cols, opens=True)
 
         compare(1, early[0])
-        for cols, ahead in zip(early, [(1, c) for c in early[1:]] + [(0, last)]):
-            compare(*ahead)
+        for i, cols in enumerate(early):
+            if i + 1 < len(early):
+                compare(1, early[i + 1])
             product(1, cols)
-            nc.scalar.copy(x_bf16[1][:, cols], x[1][:, cols])
-            project(1, cols)
+            if cols == early[-1]:
+                rounded = shared.tile([P, PIECE], BF16, name="rounded_late")
+            else:
+                rounded = held.tile([P, PIECE], BF16, name=f"rounded1_{cols.start}")
+            x_bf16[1, cols.start] = rounded[:]
+            nc.scalar.copy(rounded[:], x[1][:, cols])
+            project(1, cols, opens=False)
             for m in range(2):
                 relu_on_scalar(m, cols)
 
-        compare(1, last)
-        product(0, last)
-        nc.scalar.copy(x_bf16[0][:, last], x[0][:, last])
-        for cols in halves:
-            project(0, cols)
-        for cols in halves:
-            product(1, cols)
-        nc.scalar.copy(x_bf16[1][:, halves[0]], x[1][:, halves[0]])
-        nc.vector.tensor_copy(x_bf16[1][:, halves[1]], x[1][:, halves[1]])
-        for cols in halves:
-            project(1, cols)
+        for r in (1, 0):
+            compare(r, last)
+        steps = [(r, cols) for cols in parts for r in (1, 0)]
+        for r, cols in steps:
+            product(r, cols)
+        rounded = shared.tile([P, 2, PIECE], BF16, name="rounded_late")
+        for r, cols in steps:
+            x_bf16[r, cols.start] = rounded[:, r, cols.start - last.start : cols.stop - last.start]
+        for r, cols in steps[:-1]:
+            nc.scalar.copy(x_bf16[r, cols.start], x[r][:, cols])
+            project(r, cols, opens=(r == 1))
+        nc.vector.tensor_copy(x_bf16[0, parts[-1].start], x[0][:, parts[-1]])
+        project(0, parts[-1], opens=False)
+        for cols in parts:
             relu_on_scalar(0, cols)
             relu_on_vector(1, cols)

import concourse.mybir as mybir

P = 128
GROUP = 16
PIECE = 512
BANKS = 8
F32, BF16, U16 = mybir.dt.float32, mybir.dt.bfloat16, mybir.dt.uint16
ALU = mybir.AluOpType
ACT = mybir.ActivationFunctionType

FLOPS = 2 * 256 * 256 * 2048


def tile_lookup_sel_relu_kernel(tc, tab, th, w, b, offs, out):
    nc = tc.nc
    rows, places = tab.shape[1], tab.shape[2]
    outs, entries = out.shape
    assert rows == 2 * P and outs == 2 * P and entries == 4 * PIECE
    pieces = [slice(s, s + PIECE) for s in range(0, entries, PIECE)]
    early, last = pieces[:-1], pieces[-1]
    cuts = [last.start, last.start + PIECE // 2, last.stop - PIECE // 4, last.stop]
    parts = [slice(lo, hi) for lo, hi in zip(cuts, cuts[1:])]

    def block(i):
        return slice(i * P, (i + 1) * P)

    with (
        tc.tile_pool(name="held", bufs=1) as held,
        tc.tile_pool(name="shared", bufs=1) as shared,
        tc.psum_pool(name="psum", bufs=BANKS) as psum,
    ):
        lists = held.tile([P, entries // GROUP], U16, name="lists")
        keys = [held.tile([P, places], F32, name=f"keys{r}") for r in range(2)]
        values = [held.tile([P, places], F32, name=f"values{r}") for r in range(2)]
        limits = [held.tile([P, entries], F32, name=f"limits{r}") for r in range(2)]
        passed = [held.tile([P, entries], F32, name=f"passed{r}") for r in range(2)]
        x = [held.tile([P, entries], F32, name=f"x{r}") for r in range(2)]
        result = [held.tile([P, entries], F32, name=f"result{m}") for m in range(2)]
        weights = held.tile([P, 2, outs], BF16, name="weights")
        bias = [held.tile([P, 1], F32, name=f"bias{m}") for m in range(2)]
        x_bf16 = {}
        sums = {}

        def offsets(cols):
            return lists[:, cols.start // GROUP : cols.stop // GROUP]

        def load_limits(r, cols):
            nc.sync.dma_start(limits[r][:, cols], th[block(r), cols])

        def compare(r, cols):
            nc.vector.tensor_tensor(passed[r][:, cols], keys[r][:].indirect(offsets(cols)), limits[r][:, cols], ALU.is_ge)

        def product(r, cols):
            nc.vector.tensor_tensor(x[r][:, cols], values[r][:].indirect(offsets(cols)), passed[r][:, cols], ALU.mult)

        def project(r, cols, opens):
            for m in range(2):
                if opens:
                    sums[m, cols.start] = psum.tile([P, cols.stop - cols.start], F32, name="sums")
                nc.tensor.matmul(
                    sums[m, cols.start][:], weights[:, r, block(m)], x_bf16[r, cols.start], start=opens, stop=not opens
                )

        def relu_on_scalar(m, cols):
            nc.scalar.activation(result[m][:, cols], sums[m, cols.start][:], ACT.Relu, bias=bias[m][:])
            nc.sync.dma_start(out[block(m), cols], result[m][:, cols])

        def relu_on_vector(m, cols):
            nc.vector.tensor_scalar(result[m][:, cols], sums[m, cols.start][:], bias[m][:], 0.0, ALU.add, ALU.max)
            nc.sync.dma_start(out[block(m), cols], result[m][:, cols])

        nc.sync.dma_start(keys[0][:], tab[0, block(0), :])
        nc.sync.dma_start(lists[:], offs)
        for cols in early:
            load_limits(0, cols)
        nc.sync.dma_start(values[0][:], tab[1, block(0), :])
        nc.sync.dma_start(keys[1][:], tab[0, block(1), :])
        load_limits(1, early[0])
        load_limits(1, early[1])
        nc.sync.dma_start(values[1][:], tab[1, block(1), :])
        nc.sync.dma_start(weights[:], w.rearrange("(r p) m -> p r m", p=P))
        load_limits(1, early[2])
        for m in range(2):
            nc.sync.dma_start(bias[m][:], b[block(m), :])
        for r in (1, 0):
            load_limits(r, last)

        for cols in early:
            compare(0, cols)
        for cols in early:
            product(0, cols)
            rounded = held.tile([P, PIECE], BF16, name=f"rounded0_{cols.start}")
            x_bf16[0, cols.start] = rounded[:]
            nc.scalar.copy(rounded[:], x[0][:, cols])
            project(0, cols, opens=True)

        compare(1, early[0])
        for i, cols in enumerate(early):
            if i + 1 < len(early):
                compare(1, early[i + 1])
            product(1, cols)
            if cols == early[-1]:
                rounded = shared.tile([P, PIECE], BF16, name="rounded_late")
            else:
                rounded = held.tile([P, PIECE], BF16, name=f"rounded1_{cols.start}")
            x_bf16[1, cols.start] = rounded[:]
            nc.scalar.copy(rounded[:], x[1][:, cols])
            project(1, cols, opens=False)
            for m in range(2):
                relu_on_scalar(m, cols)

        for r in (1, 0):
            compare(r, last)
        steps = [(r, cols) for cols in parts for r in (1, 0)]
        for r, cols in steps:
            product(r, cols)
        rounded = shared.tile([P, 2, PIECE], BF16, name="rounded_late")
        for r, cols in steps:
            x_bf16[r, cols.start] = rounded[:, r, cols.start - last.start : cols.stop - last.start]
        for r, cols in steps[:-1]:
            nc.scalar.copy(x_bf16[r, cols.start], x[r][:, cols])
            project(r, cols, opens=(r == 1))
        nc.vector.tensor_copy(x_bf16[0, parts[-1].start], x[0][:, parts[-1]])
        project(0, parts[-1], opens=False)
        for cols in parts:
            relu_on_scalar(0, cols)
            relu_on_vector(1, cols)
